import numpy as np
import ml_dtypes


def mxq(x, axis, fmt="e4m3"):
    dtype, down = {"e4m3": (ml_dtypes.float8_e4m3fn, 7), "e5m2": (ml_dtypes.float8_e5m2, 14)}[fmt]
    v = np.moveaxis(np.asarray(x, np.float32).astype(ml_dtypes.bfloat16).astype(np.float64), axis, -1)
    blocks = v.reshape(v.shape[:-1] + (-1, 32))
    amax = np.abs(blocks).max(-1, keepdims=True)
    byte = np.maximum(np.where(amax > 0, np.frexp(amax)[1] - 1 + 127, 0) - down, 1)
    scale = np.exp2(byte - 127.0)
    codes = (blocks / scale).astype(np.float32).astype(dtype).astype(np.float64)
    return np.moveaxis((codes * scale).reshape(v.shape), -1, axis)


WIDE = False


def mx_kscale(k):
    if not WIDE:
        return np.ones(k)
    levels = np.array([10, -10, 5, -5, 0])
    if k % 512:
        return np.exp2(np.random.permutation(np.resize(levels, k // 32))).repeat(32)
    a = np.empty((k // 512, 16))
    for p in range(k // 512):
        a[p, :8] = np.random.permutation(np.resize(levels, 8))
        for g in range(8):
            far = levels[np.abs(levels - a[p, g]) >= 10]
            a[p, g + 8] = far[np.random.randint(len(far))]
    return np.exp2(a.ravel()).repeat(32)


def f64(x):
    return np.asarray(x).astype(np.float64)


def striped(idx):
    return np.tile(idx.reshape(-1, 16).T, (8, 1)).astype(np.uint16)


def unstriped(offs):
    return offs[:16].T.reshape(-1).astype(np.int64)


def striped8(idx):
    return np.concatenate([x.reshape(-1, 16).T for x in idx]).astype(np.uint16)


def runs(offs, k):
    lists = np.stack([offs[16 * r : 16 * r + 16].T.reshape(-1) for r in range(8)]).astype(np.int64)
    return lists[np.arange(k) % 512 // 64]


def pack_weight(w):
    k, n = w.shape
    w = f64(np.asarray(w, np.float32).astype(ml_dtypes.bfloat16)).reshape(k // 32, 32, n)
    amax = np.abs(w).max(1)
    byte = np.clip(np.where(amax > 0, np.frexp(amax)[1] - 1 + 127 - 7, 1), 1, 254)
    scaled = (w * np.exp2(127.0 - byte)[:, None, :]).reshape(k, n).astype(np.float32)
    words = np.ascontiguousarray(scaled.reshape(k // 512, 128, 4, n).transpose(0, 1, 3, 2)).astype(ml_dtypes.float8_e4m3fn).view(np.uint8)
    return words, np.ascontiguousarray(byte.astype(np.uint8).reshape(k // 512, 16, n))


def unpack_weight(words, scales):
    g, p, n, _ = words.shape
    vals = np.ascontiguousarray(words).view(ml_dtypes.float8_e4m3fn).astype(np.float64) * np.repeat(np.exp2(scales.astype(np.float64) - 127.0), 8, axis=1)[..., None]
    return vals.transpose(0, 1, 3, 2).reshape(g * 512, n)


K, T, S, N, G, H = 512, 1024, 512, 512, 2048, 512


def setup_inputs():
    n = np.random.standard_normal
    s = mx_kscale(K)[:, None]
    u = mx_kscale(S)
    packed_xT = pack_weight(n((K, T)) * s)
    packed_dT = pack_weight(n((K, G)) / s)
    return {
        "x_words": packed_xT[0],
        "x_scales": packed_xT[1],
        "d_words": packed_dT[0],
        "d_scales": packed_dT[1],
        "gn": (np.random.uniform(0.5, 1.5, (H, 1)) * u[:, None]).astype(np.float32),
        "w1": (n((H, N)) / np.sqrt(H) / u[:, None]).astype(np.float32),
        "offs": striped(np.random.permutation(T)[:S]),
        "k1": striped8(np.random.randint(0, G, (8, H))),
        "two": striped(np.random.permutation(T)[:S]),
        "k2": striped8(np.random.randint(0, G, (8, H))),
        "n1": striped8(np.stack([np.random.permutation(S) for _ in range(8)])),
        "n2": striped8(np.stack([np.random.permutation(S) for _ in range(8)])),
        "n3": striped8(np.stack([np.random.permutation(S) for _ in range(8)])),
    }


def reference(x_words, x_scales, d_words, d_scales, gn, w1, offs, k1, two, k2, n1, n2, n3):
    d_k1 = unpack_weight(d_words, d_scales)[np.arange(K)[:, None], runs(k1, K)]
    xq = unpack_weight(x_words, x_scales)[:, unstriped(offs)]
    a = 0.0625 * (d_k1.T @ xq)
    d_k2 = unpack_weight(d_words, d_scales)[np.arange(K)[:, None], runs(k2, K)]
    x_two = unpack_weight(x_words, x_scales)[:, unstriped(two)]
    b = 0.0625 * (d_k2.T @ x_two)
    z = f64(gn) * (0.75 * (a * (b[np.arange(H)[:, None], runs(n2, H)]) - ((a[np.arange(H)[:, None], runs(n1, H)]) * b)))
    h = mxq(f64(w1), 0, "e4m3").T @ mxq(z, 0, "e4m3")
    return h - (h[np.arange(N)[:, None], runs(n3, N)])

@@ -1,0 +1,209 @@
+from contextlib import ExitStack
+
+import concourse.mybir as mybir
+from concourse.masks import make_identity
+
+K, T, S, N, G, H = 512, 1024, 512, 512, 2048, 512
+FLOPS = 2 * K * H * S * 2 + 2 * H * N * S
+
+F32 = mybir.dt.float32
+BF16 = mybir.dt.bfloat16
+I32 = mybir.dt.int32
+U32 = mybir.dt.uint32
+U16 = mybir.dt.uint16
+U8 = mybir.dt.uint8
+FP8X4 = mybir.dt.float8_e4m3fn_x4
+COPY = mybir.ActivationFunctionType.Copy
+MULT = mybir.AluOpType.mult
+SUB = mybir.AluOpType.subtract
+
+P = 128
+PACK = 4
+RUN = 8
+HALF = S // 2
+LIST_HALF = HALF // 16
+CONST = 0.75 * 0.0625 * 0.0625
+
+
+def tile_picked_twpqcrossbdif_none_p_kernel(tc, x_words, x_scales, d_words, d_scales, gn, w1, offs, k1, two, k2, n1, n2, n3, out):
+    nc = tc.nc
+    with ExitStack() as ctx:
+        keep = ctx.enter_context(tc.tile_pool(name="keep", bufs=1))
+        psum = ctx.enter_context(tc.psum_pool(name="psum", bufs=1))
+
+        def load_list(src, name):
+            tile = keep.tile([P, S // 16], U16, name=name)
+            nc.sync.dma_start(tile[:], src)
+            return tile
+
+        d_bytes = keep.tile([P, G], U8, name="d_bytes")
+        x_bytes = keep.tile([P, T], U8, name="x_bytes")
+        d_table = keep.tile([P, G], U32, name="d_table")
+        x_table = keep.tile([P, T], U32, name="x_table")
+        def scale_rows(scales):
+            rows = scales[0].bitcast(I32)
+            return rows.unsqueeze(1).to_broadcast([16, RUN, rows.shape[1]])
+
+        k1_l = load_list(k1, "k1_l")
+        nc.sync.dma_start(d_bytes[:].bitcast(I32), scale_rows(d_scales))
+        offs_l = load_list(offs, "offs_l")
+        nc.sync.dma_start(x_bytes[:].bitcast(I32), scale_rows(x_scales))
+        nc.sync.dma_start(d_table[:].bitcast(I32), d_words[0].rearrange("p n t -> p (n t)").bitcast(I32))
+        nc.sync.dma_start(x_table[:].bitcast(I32), x_words[0].rearrange("p n t -> p (n t)").bitcast(I32))
+        k2_l = load_list(k2, "k2_l")
+        two_l = load_list(two, "two_l")
+        n1_l = load_list(n1, "n1_l")
+        n2_l = load_list(n2, "n2_l")
+        n3_l = load_list(n3, "n3_l")
+        w_raw = keep.tile([P, PACK, N], F32, name="w_raw")
+        w_rows = w1.rearrange("(g t r) n -> t g r n", t=PACK, r=RUN)
+        for t in range(PACK):
+            nc.sync.dma_start(w_raw[:, t, :], w_rows[t])
+
+        gn_rows = keep.tile([P, P], F32, name="gn_rows")
+        identity = keep.tile([P, P], F32, name="identity")
+        nc.gpsimd.memset(gn_rows[:], 0.0)
+        nc.gpsimd.dma_start(
+            gn_rows[0:PACK, :].rearrange("t (g r) -> t g r", r=RUN),
+            gn.rearrange("(g t r) o -> t g (r o)", t=PACK, r=RUN),
+        )
+        make_identity(nc, identity[:])
+        gn_turned = psum.tile([P, P], F32, name="gn_turned", tag="b3")
+        nc.tensor.transpose(gn_turned[:], gn_rows[:], identity[:])
+        gain = keep.tile([P, PACK], F32, name="gain")
+        nc.scalar.activation(gain[:], gn_turned[:, 0:PACK], COPY, scale=CONST)
+
+        def coded_product(name, d_list, x_list, queue):
+            d_picked_bytes = keep.tile([P, H], U8, name=name + "_d_bytes")
+            x_picked_bytes = keep.tile([P, S], U8, name=name + "_x_bytes")
+            planes = keep.tile([P, H + S], U8, name=name + "_planes", align_bytes=64)
+            nc.vector.tensor_copy(d_picked_bytes[:], d_bytes[:].indirect(d_list[:]))
+            nc.vector.tensor_copy(x_picked_bytes[:], x_bytes[:].indirect(x_list[:]))
+            nc.vector.tensor_copy(
+                planes[:, 0:H].bitcast(I32).rearrange("p (t g r) -> p t g r", t=PACK, r=RUN // 4),
+                d_picked_bytes[:].bitcast(I32).rearrange("p (g t r) -> p t g r", t=PACK, r=RUN // 4),
+            )
+            nc.vector.tensor_copy(planes[:, H : H + S].bitcast(I32), x_picked_bytes[:].bitcast(I32))
+            for row in range(1, 4):
+                queue.dma_start(planes[row:P:32, :].bitcast(I32), planes[RUN * row : P : 32, :].bitcast(I32))
+            d_picked = keep.tile([P, H], U32, name=name + "_d_words")
+            d_dealt = keep.tile([P, H], U32, name=name + "_d_dealt", align_bytes=64)
+            x_picked = keep.tile([P, S], U32, name=name + "_x_words", align_bytes=64)
+            nc.vector.tensor_copy(d_picked[:], d_table[:].indirect(d_list[:]))
+            nc.vector.tensor_copy(x_picked[:], x_table[:].indirect(x_list[:]))
+            nc.vector.tensor_copy(
+                d_dealt[:].rearrange("p (t g r) -> p t g r", t=PACK, r=RUN),
+                d_picked[:].rearrange("p (g t r) -> p t g r", t=PACK, r=RUN),
+            )
+            banks = []
+            for t in range(PACK):
+                bank = psum.tile([P, S], F32, name=name + str(t), tag=name + str(t))
+                cols = slice(t * P, (t + 1) * P)
+                nc.tensor.matmul_mx(
+                    out=bank[:],
+                    lhsT=d_dealt[:, cols].bitcast(FP8X4),
+                    lhsT_scale=planes[:, cols],
+                    rhs=x_picked[:].bitcast(FP8X4),
+                    rhs_scale=planes[:, H : H + S],
+                    start=True,
+                    stop=True,
+                )
+                banks.append(bank)
+            return banks
+
+        a_banks = coded_product("a", k1_l, offs_l, nc.scalar)
+        b_banks = coded_product("b", k2_l, two_l, nc.sync)
+
+        def half_cols(half):
+            return slice(half * HALF, (half + 1) * HALF)
+
+        def looked_up(window, lists, half):
+            return window[:].indirect(lists[:, half * LIST_HALF : (half + 1) * LIST_HALF])
+
+        a_rows = [keep.tile([P, S], F32, name="a_rows%d" % t) for t in range(PACK)]
+        b_rows = [keep.tile([P, S], F32, name="b_rows%d" % t) for t in range(PACK)]
+        h_rows = [keep.tile([P, S], F32, name="h_rows%d" % t) for t in range(PACK)]
+        a_far = {}
+        for t in range(PACK):
+            nc.scalar.activation(a_rows[t][:], a_banks[t][:], COPY, scale=gain[:, t : t + 1])
+
+        def fetch_a(half, t):
+            a_far[half, t] = keep.tile([P, HALF], F32, name="a_far%d%d" % (half, t))
+            nc.scalar.activation(a_far[half, t][:], looked_up(a_rows[t], n1_l, half), COPY)
+
+        for t in range(PACK):
+            fetch_a(0, t)
+        fetch_a(1, 0)
+
+        w_grouped = keep.tile([P, PACK, P, PACK], BF16, name="w_grouped", align_bytes=64)
+        for t in range(PACK):
+            nc.vector.tensor_copy(
+                w_grouped[:, t].rearrange("p (g s i) j -> p g s j i", s=2, i=4),
+                w_raw[:].rearrange("p j (g t s i) -> p t g s j i", t=PACK, s=2, i=4)[:, t],
+            )
+        w_codes = keep.tile([P, N], U32, name="w_codes", align_bytes=64)
+        w_scales = keep.tile([P, N], U8, name="w_scales", align_bytes=64)
+        nc.vector.quantize_mx(
+            out=w_codes[:].bitcast(FP8X4), scales=w_scales[:], in_=w_grouped[:].rearrange("p t m j -> p (t m j)")
+        )
+
+        h_banks = {}
+        for half in range(2):
+            cols = half_cols(half)
+            plus = keep.tile([P, PACK, HALF], F32, name="plus%d" % half)
+            minus = keep.tile([P, PACK, HALF], F32, name="minus%d" % half)
+            for t in range(PACK):
+                if half == 0:
+                    nc.vector.tensor_copy(b_rows[t][:], b_banks[t][:])
+                elif t > 0:
+                    fetch_a(half, t)
+                nc.vector.tensor_tensor(minus[:, t, :], b_banks[t][:, cols], a_far[half, t][:], MULT)
+                if t == PACK - 1 and half == 1:
+                    nc.vector.tensor_tensor(plus[:, t, :], looked_up(b_rows[t], n2_l, half), a_rows[t][:, cols], MULT)
+                else:
+                    b_far = keep.tile([P, HALF], F32, name="b_far%d%d" % (half, t))
+                    nc.scalar.activation(b_far[:], looked_up(b_rows[t], n2_l, half), COPY)
+                    nc.vector.tensor_tensor(plus[:, t, :], b_far[:], a_rows[t][:, cols], MULT)
+            z_grouped = keep.tile([P, HALF, PACK], BF16, name="z_grouped%d" % half, align_bytes=64)
+            nc.vector.tensor_tensor(
+                z_grouped[:].rearrange("p (c i) t -> p c t i", i=4),
+                plus[:].rearrange("p t (c i) -> p c t i", i=4),
+                minus[:].rearrange("p t (c i) -> p c t i", i=4),
+                SUB,
+            )
+            z_codes = keep.tile([P, HALF], U32, name="z_codes%d" % half, align_bytes=64)
+            z_scales = keep.tile([P, HALF], U8, name="z_scales%d" % half, align_bytes=64)
+            nc.vector.quantize_mx(
+                out=z_codes[:].bitcast(FP8X4), scales=z_scales[:], in_=z_grouped[:].rearrange("p c t -> p (c t)")
+            )
+            for t in range(PACK):
+                tag = "ab"[half] + str(t)
+                bank = psum.tile([P, HALF], F32, name="h%d%d" % (half, t), tag=tag)
+                w_cols = slice(t * P, (t + 1) * P)
+                nc.tensor.matmul_mx(
+                    out=bank[:],
+                    lhsT=w_codes[:, w_cols].bitcast(FP8X4),
+                    lhsT_scale=w_scales[:, w_cols],
+                    rhs=z_codes[:].bitcast(FP8X4),
+                    rhs_scale=z_scales[:],
+                    start=True,
+                    stop=True,
+                )
+                h_banks[half, t] = bank
+            for t in range(PACK):
+                if half == 1 and t % 2 == 1:
+                    nc.vector.tensor_copy(h_rows[t][:, cols], h_banks[half, t][:])
+                else:
+                    nc.scalar.copy(h_rows[t][:, cols], h_banks[half, t][:])
+
+        out_rows = out.rearrange("(g t r) n -> t g r n", t=PACK, r=RUN)
+        for t in (0, 1, 2, 3):
+            for half in range(2):
+                h_far = keep.tile([P, HALF], F32, name="h_far%d%d" % (half, t))
+                if t == 1:
+                    nc.vector.tensor_copy(h_far[:], looked_up(h_rows[t], n3_l, half))
+                else:
+                    nc.scalar.activation(h_far[:], looked_up(h_rows[t], n3_l, half), COPY)
+                result = keep.tile([P, HALF], F32, name="result%d%d" % (half, t))
+                nc.vector.tensor_tensor(result[:], h_banks[half, t][:], h_far[:], SUB)
+                nc.sync.dma_start(out_rows[t][:, :, half_cols(half)], result[:])

@@ -15,6 +15,7 @@ U8 = mybir.dt.uint8
 FP8X4 = mybir.dt.float8_e4m3fn_x4
 COPY = mybir.ActivationFunctionType.Copy
 MULT = mybir.AluOpType.mult
+ADD = mybir.AluOpType.add
 SUB = mybir.AluOpType.subtract
 
 P = 128
@@ -29,6 +30,7 @@ def tile_picked_twpqcrossbdif_none_p_kernel(tc, x_words, x_scales, d_words, d_sc
     nc = tc.nc
     with ExitStack() as ctx:
         keep = ctx.enter_context(tc.tile_pool(name="keep", bufs=1))
+        shared = ctx.enter_context(tc.tile_pool(name="shared", bufs=1))
         psum = ctx.enter_context(tc.psum_pool(name="psum", bufs=1))
 
         def load_list(src, name):
@@ -44,26 +46,22 @@ def tile_picked_twpqcrossbdif_none_p_kernel(tc, x_words, x_scales, d_words, d_sc
             rows = scales[0].bitcast(I32)
             return rows.unsqueeze(1).to_broadcast([16, RUN, rows.shape[1]])
 
-        k1_l = load_list(k1, "k1_l")
-        nc.sync.dma_start(d_bytes[:].bitcast(I32), scale_rows(d_scales))
-        offs_l = load_list(offs, "offs_l")
         nc.sync.dma_start(x_bytes[:].bitcast(I32), scale_rows(x_scales))
+        offs_l = load_list(offs, "offs_l")
+        nc.sync.dma_start(d_bytes[:].bitcast(I32), scale_rows(d_scales))
+        k1_l = load_list(k1, "k1_l")
         nc.sync.dma_start(d_table[:].bitcast(I32), d_words[0].rearrange("p n t -> p (n t)").bitcast(I32))
-        nc.sync.dma_start(x_table[:].bitcast(I32), x_words[0].rearrange("p n t -> p (n t)").bitcast(I32))
-        k2_l = load_list(k2, "k2_l")
-        two_l = load_list(two, "two_l")
         n1_l = load_list(n1, "n1_l")
         n2_l = load_list(n2, "n2_l")
+        nc.sync.dma_start(x_table[:].bitcast(I32), x_words[0].rearrange("p n t -> p (n t)").bitcast(I32))
+        two_l = load_list(two, "two_l")
+        k2_l = load_list(k2, "k2_l")
         n3_l = load_list(n3, "n3_l")
-        w_raw = keep.tile([P, PACK, N], F32, name="w_raw")
-        w_rows = w1.rearrange("(g t r) n -> t g r n", t=PACK, r=RUN)
-        for t in range(PACK):
-            nc.sync.dma_start(w_raw[:, t, :], w_rows[t])
 
         gn_rows = keep.tile([P, P], F32, name="gn_rows")
         identity = keep.tile([P, P], F32, name="identity")
         nc.gpsimd.memset(gn_rows[:], 0.0)
-        nc.gpsimd.dma_start(
+        nc.scalar.dma_start(
             gn_rows[0:PACK, :].rearrange("t (g r) -> t g r", r=RUN),
             gn.rearrange("(g t r) o -> t g (r o)", t=PACK, r=RUN),
         )
@@ -73,22 +71,24 @@ def tile_picked_twpqcrossbdif_none_p_kernel(tc, x_words, x_scales, d_words, d_sc
         gain = keep.tile([P, PACK], F32, name="gain")
         nc.scalar.activation(gain[:], gn_turned[:, 0:PACK], COPY, scale=CONST)
 
-        def coded_product(name, d_list, x_list, queue):
-            d_picked_bytes = keep.tile([P, H], U8, name=name + "_d_bytes")
-            x_picked_bytes = keep.tile([P, S], U8, name=name + "_x_bytes")
+        def coded_product(name, d_list, x_list, base):
+            d_picked_bytes = shared.tile([P, H], U8, name=name + "_d_bytes", offset=base + 4 * H - H // 2)
+            x_picked_bytes = keep.tile([P, S], U8, name=name + "_x_bytes", tag=name + "_x_bytes")
+            staged = keep.tile([P, H + S], U8, name=name + "_staged", tag=name + "_staged")
             planes = keep.tile([P, H + S], U8, name=name + "_planes", align_bytes=64)
-            nc.vector.tensor_copy(d_picked_bytes[:], d_bytes[:].indirect(d_list[:]))
+            nc.gpsimd.memset(planes[:].bitcast(I32), 0)
             nc.vector.tensor_copy(x_picked_bytes[:], x_bytes[:].indirect(x_list[:]))
+            nc.vector.tensor_copy(d_picked_bytes[:], d_bytes[:].indirect(d_list[:]))
+            nc.vector.tensor_copy(staged[:, H : H + S].bitcast(I32), x_picked_bytes[:].bitcast(I32))
             nc.vector.tensor_copy(
-                planes[:, 0:H].bitcast(I32).rearrange("p (t g r) -> p t g r", t=PACK, r=RUN // 4),
+                staged[:, 0:H].bitcast(I32).rearrange("p (t g r) -> p t g r", t=PACK, r=RUN // 4),
                 d_picked_bytes[:].bitcast(I32).rearrange("p (g t r) -> p t g r", t=PACK, r=RUN // 4),
             )
-            nc.vector.tensor_copy(planes[:, H : H + S].bitcast(I32), x_picked_bytes[:].bitcast(I32))
-            for row in range(1, 4):
-                queue.dma_start(planes[row:P:32, :].bitcast(I32), planes[RUN * row : P : 32, :].bitcast(I32))
-            d_picked = keep.tile([P, H], U32, name=name + "_d_words")
-            d_dealt = keep.tile([P, H], U32, name=name + "_d_dealt", align_bytes=64)
-            x_picked = keep.tile([P, S], U32, name=name + "_x_words", align_bytes=64)
+            for q in range(0, P, 32):
+                nc.sync.dma_start(planes[q : q + 4, :].bitcast(I32), staged[q : q + 32 : RUN, :].bitcast(I32))
+            d_picked = shared.tile([P, H], U32, name=name + "_d_words", offset=base)
+            d_dealt = keep.tile([P, H], U32, name=name + "_d_dealt", tag=name + "_d_dealt", align_bytes=64)
+            x_picked = shared.tile([P, S], U32, name=name + "_x_words", offset=base + 4 * H, align_bytes=64)
             nc.vector.tensor_copy(d_picked[:], d_table[:].indirect(d_list[:]))
             nc.vector.tensor_copy(x_picked[:], x_table[:].indirect(x_list[:]))
             nc.vector.tensor_copy(
@@ -111,8 +111,12 @@ def tile_picked_twpqcrossbdif_none_p_kernel(tc, x_words, x_scales, d_words, d_sc
                 banks.append(bank)
             return banks
 
-        a_banks = coded_product("a", k1_l, offs_l, nc.scalar)
-        b_banks = coded_product("b", k2_l, two_l, nc.sync)
+        a_banks = coded_product("a", k1_l, offs_l, 0)
+        w_raw = keep.tile([P, PACK, N], F32, name="w_raw", tag="a_staged")
+        w_rows = w1.rearrange("(g t r) n -> t g r n", t=PACK, r=RUN)
+        for t in range(PACK):
+            nc.sync.dma_start(w_raw[:, t, :], w_rows[t])
+        b_banks = coded_product("b", k2_l, two_l, 4 * (H + S))
 
         def half_cols(half):
             return slice(half * HALF, (half + 1) * HALF)
@@ -123,52 +127,34 @@ def tile_picked_twpqcrossbdif_none_p_kernel(tc, x_words, x_scales, d_words, d_sc
         a_rows = [keep.tile([P, S], F32, name="a_rows%d" % t) for t in range(PACK)]
         b_rows = [keep.tile([P, S], F32, name="b_rows%d" % t) for t in range(PACK)]
         h_rows = [keep.tile([P, S], F32, name="h_rows%d" % t) for t in range(PACK)]
-        a_far = {}
         for t in range(PACK):
             nc.scalar.activation(a_rows[t][:], a_banks[t][:], COPY, scale=gain[:, t : t + 1])
 
-        def fetch_a(half, t):
-            a_far[half, t] = keep.tile([P, HALF], F32, name="a_far%d%d" % (half, t))
-            nc.scalar.activation(a_far[half, t][:], looked_up(a_rows[t], n1_l, half), COPY)
+        def fetch(engine, name, rows, lists, half, t):
+            far = keep.tile([P, HALF], F32, name="%s_far%d%d" % (name, half, t))
+            if engine is nc.scalar:
+                nc.scalar.activation(far[:], looked_up(rows[t], lists, half), COPY)
+            else:
+                nc.vector.tensor_copy(far[:], looked_up(rows[t], lists, half))
+            return far
 
-        for t in range(PACK):
-            fetch_a(0, t)
-        fetch_a(1, 0)
-
-        w_grouped = keep.tile([P, PACK, P, PACK], BF16, name="w_grouped", align_bytes=64)
-        for t in range(PACK):
-            nc.vector.tensor_copy(
-                w_grouped[:, t].rearrange("p (g s i) j -> p g s j i", s=2, i=4),
-                w_raw[:].rearrange("p j (g t s i) -> p t g s j i", t=PACK, s=2, i=4)[:, t],
-            )
-        w_codes = keep.tile([P, N], U32, name="w_codes", align_bytes=64)
-        w_scales = keep.tile([P, N], U8, name="w_scales", align_bytes=64)
-        nc.vector.quantize_mx(
-            out=w_codes[:].bitcast(FP8X4), scales=w_scales[:], in_=w_grouped[:].rearrange("p t m j -> p (t m j)")
-        )
-
+        plus = [keep.tile([P, PACK, HALF], F32, name="plus%d" % half) for half in range(2)]
+        minus = [keep.tile([P, PACK, HALF], F32, name="minus%d" % half) for half in range(2)]
         h_banks = {}
-        for half in range(2):
-            cols = half_cols(half)
-            plus = keep.tile([P, PACK, HALF], F32, name="plus%d" % half)
-            minus = keep.tile([P, PACK, HALF], F32, name="minus%d" % half)
-            for t in range(PACK):
-                if half == 0:
-                    nc.vector.tensor_copy(b_rows[t][:], b_banks[t][:])
-                elif t > 0:
-                    fetch_a(half, t)
-                nc.vector.tensor_tensor(minus[:, t, :], b_banks[t][:, cols], a_far[half, t][:], MULT)
-                if t == PACK - 1 and half == 1:
-                    nc.vector.tensor_tensor(plus[:, t, :], looked_up(b_rows[t], n2_l, half), a_rows[t][:, cols], MULT)
-                else:
-                    b_far = keep.tile([P, HALF], F32, name="b_far%d%d" % (half, t))
-                    nc.scalar.activation(b_far[:], looked_up(b_rows[t], n2_l, half), COPY)
-                    nc.vector.tensor_tensor(plus[:, t, :], b_far[:], a_rows[t][:, cols], MULT)
+
+        def make_minus(half, t, a_far):
+            nc.vector.tensor_tensor(minus[half][:, t, :], b_banks[t][:, half_cols(half)], a_far[:], MULT)
+
+        def make_plus(half, t):
+            b_far = fetch(nc.scalar, "b", b_rows, n2_l, half, t)
+            nc.vector.tensor_tensor(plus[half][:, t, :], b_far[:], a_rows[t][:, half_cols(half)], MULT)
+
+        def dense_layer(half):
             z_grouped = keep.tile([P, HALF, PACK], BF16, name="z_grouped%d" % half, align_bytes=64)
             nc.vector.tensor_tensor(
                 z_grouped[:].rearrange("p (c i) t -> p c t i", i=4),
-                plus[:].rearrange("p t (c i) -> p c t i", i=4),
-                minus[:].rearrange("p t (c i) -> p c t i", i=4),
+                plus[half][:].rearrange("p t (c i) -> p c t i", i=4),
+                minus[half][:].rearrange("p t (c i) -> p c t i", i=4),
                 SUB,
             )
             z_codes = keep.tile([P, HALF], U32, name="z_codes%d" % half, align_bytes=64)
@@ -177,8 +163,7 @@ def tile_picked_twpqcrossbdif_none_p_kernel(tc, x_words, x_scales, d_words, d_sc
                 out=z_codes[:].bitcast(FP8X4), scales=z_scales[:], in_=z_grouped[:].rearrange("p c t -> p (c t)")
             )
             for t in range(PACK):
-                tag = "ab"[half] + str(t)
-                bank = psum.tile([P, HALF], F32, name="h%d%d" % (half, t), tag=tag)
+                bank = psum.tile([P, HALF], F32, name="h%d%d" % (half, t), tag="ab"[half] + str(t))
                 w_cols = slice(t * P, (t + 1) * P)
                 nc.tensor.matmul_mx(
                     out=bank[:],
@@ -190,20 +175,52 @@ def tile_picked_twpqcrossbdif_none_p_kernel(tc, x_words, x_scales, d_words, d_sc
                     stop=True,
                 )
                 h_banks[half, t] = bank
-            for t in range(PACK):
-                if half == 1 and t % 2 == 1:
-                    nc.vector.tensor_copy(h_rows[t][:, cols], h_banks[half, t][:])
-                else:
-                    nc.scalar.copy(h_rows[t][:, cols], h_banks[half, t][:])
+
+        last = PACK - 1
+
+        def make_plus_fused(half, t):
+            nc.vector.tensor_tensor(plus[half][:, t, :], looked_up(b_rows[t], n2_l, half), a_rows[t][:, half_cols(half)], MULT)
+
+        a_far = {(0, t): fetch(nc.scalar, "a", a_rows, n1_l, 0, t) for t in range(PACK)}
+        a_far[1, 0] = fetch(nc.scalar, "a", a_rows, n1_l, 1, 0)
+        w_grouped = shared.tile([P, PACK, P, PACK], BF16, name="w_grouped", offset=4 * H, align_bytes=64)
+        for t in range(PACK):
+            nc.vector.tensor_copy(
+                w_grouped[:, t].rearrange("p (g s i) j -> p g s j i", s=2, i=4),
+                w_raw[:].rearrange("p j (g t s i) -> p t g s j i", t=PACK, s=2, i=4)[:, t],
+            )
+        w_codes = keep.tile([P, N], U32, name="w_codes", align_bytes=64)
+        w_scales = keep.tile([P, N], U8, name="w_scales", align_bytes=64)
+
+        nc.vector.quantize_mx(
+            out=w_codes[:].bitcast(FP8X4), scales=w_scales[:], in_=w_grouped[:].rearrange("p t m j -> p (t m j)")
+        )
+        for t in range(PACK):
+            nc.scalar.copy(b_rows[t][:], b_banks[t][:])
+            make_minus(0, t, a_far[0, t])
+            if t < last:
+                make_plus(0, t)
+        make_minus(1, 0, a_far[1, 0])
+        make_plus_fused(0, last)
+        dense_layer(0)
+        for t in range(1, PACK):
+            make_minus(1, t, fetch(nc.scalar, "a", a_rows, n1_l, 1, t))
+        make_plus_fused(1, last)
+        for t in range(last):
+            make_plus(1, t)
+        for t in range(PACK):
+            nc.scalar.copy(h_rows[t][:, half_cols(0)], h_banks[0, t][:])
+        dense_layer(1)
+        for t in range(PACK):
+            if t % 2 == 1:
+                nc.vector.tensor_copy(h_rows[t][:, half_cols(1)], h_banks[1, t][:])
+            else:
+                nc.scalar.copy(h_rows[t][:, half_cols(1)], h_banks[1, t][:])
 
         out_rows = out.rearrange("(g t r) n -> t g r n", t=PACK, r=RUN)
-        for t in (0, 1, 2, 3):
+        for t in range(PACK):
             for half in range(2):
-                h_far = keep.tile([P, HALF], F32, name="h_far%d%d" % (half, t))
-                if t == 1:
-                    nc.vector.tensor_copy(h_far[:], looked_up(h_rows[t], n3_l, half))
-                else:
-                    nc.scalar.activation(h_far[:], looked_up(h_rows[t], n3_l, half), COPY)
+                h_far = fetch(nc.vector if t == 1 else nc.scalar, "h", h_rows, n3_l, half, t)
                 result = keep.tile([P, HALF], F32, name="result%d%d" % (half, t))
                 nc.vector.tensor_tensor(result[:], h_banks[half, t][:], h_far[:], SUB)
                 nc.sync.dma_start(out_rows[t][:, :, half_cols(half)], result[:])

@@ -15,15 +15,26 @@ U8 = mybir.dt.uint8
 FP8X4 = mybir.dt.float8_e4m3fn_x4
 COPY = mybir.ActivationFunctionType.Copy
 MULT = mybir.AluOpType.mult
-ADD = mybir.AluOpType.add
 SUB = mybir.AluOpType.subtract
 
 P = 128
+QUADRANT = 32
 PACK = 4
 RUN = 8
+LIST_ROWS = 16
+SCALE_ROWS = K // 32
+LINE = 4
 HALF = S // 2
-LIST_HALF = HALF // 16
+LAST = PACK - 1
 CONST = 0.75 * 0.0625 * 0.0625
+EARLY = 2
+
+WORDS = PACK * H
+A_WORDS_AT = 0
+B_WORDS_AT = 2 * WORDS
+A_BYTES_AT = 4 * WORDS
+B_BYTES_AT = B_WORDS_AT + WORDS - H // 2
+W_GROUPED_AT = A_WORDS_AT + WORDS
 
 
 def tile_picked_twpqcrossbdif_none_p_kernel(tc, x_words, x_scales, d_words, d_scales, gn, w1, offs, k1, two, k2, n1, n2, n3, out):
@@ -34,29 +45,33 @@ def tile_picked_twpqcrossbdif_none_p_kernel(tc, x_words, x_scales, d_words, d_sc
         psum = ctx.enter_context(tc.psum_pool(name="psum", bufs=1))
 
         def load_list(src, name):
-            tile = keep.tile([P, S // 16], U16, name=name)
+            tile = keep.tile([P, S // LIST_ROWS], U16, name=name)
             nc.sync.dma_start(tile[:], src)
             return tile
+
+        def scale_rows(scales):
+            rows = scales[0].bitcast(I32)
+            return rows.unsqueeze(1).to_broadcast([SCALE_ROWS, RUN, rows.shape[1]])
+
+        def packed_words(words):
+            return words[0].rearrange("p n t -> p (n t)").bitcast(I32)
 
         d_bytes = keep.tile([P, G], U8, name="d_bytes")
         x_bytes = keep.tile([P, T], U8, name="x_bytes")
         d_table = keep.tile([P, G], U32, name="d_table")
         x_table = keep.tile([P, T], U32, name="x_table")
-        def scale_rows(scales):
-            rows = scales[0].bitcast(I32)
-            return rows.unsqueeze(1).to_broadcast([16, RUN, rows.shape[1]])
 
         nc.sync.dma_start(x_bytes[:].bitcast(I32), scale_rows(x_scales))
-        offs_l = load_list(offs, "offs_l")
+        offs_list = load_list(offs, "offs_list")
         nc.sync.dma_start(d_bytes[:].bitcast(I32), scale_rows(d_scales))
-        k1_l = load_list(k1, "k1_l")
-        nc.sync.dma_start(d_table[:].bitcast(I32), d_words[0].rearrange("p n t -> p (n t)").bitcast(I32))
-        n1_l = load_list(n1, "n1_l")
-        n2_l = load_list(n2, "n2_l")
-        nc.sync.dma_start(x_table[:].bitcast(I32), x_words[0].rearrange("p n t -> p (n t)").bitcast(I32))
-        two_l = load_list(two, "two_l")
-        k2_l = load_list(k2, "k2_l")
-        n3_l = load_list(n3, "n3_l")
+        k1_list = load_list(k1, "k1_list")
+        nc.sync.dma_start(d_table[:].bitcast(I32), packed_words(d_words))
+        n1_list = load_list(n1, "n1_list")
+        n2_list = load_list(n2, "n2_list")
+        nc.sync.dma_start(x_table[:].bitcast(I32), packed_words(x_words))
+        two_list = load_list(two, "two_list")
+        k2_list = load_list(k2, "k2_list")
+        n3_list = load_list(n3, "n3_list")
 
         gn_rows = keep.tile([P, P], F32, name="gn_rows")
         identity = keep.tile([P, P], F32, name="identity")
@@ -66,95 +81,108 @@ def tile_picked_twpqcrossbdif_none_p_kernel(tc, x_words, x_scales, d_words, d_sc
             gn.rearrange("(g t r) o -> t g (r o)", t=PACK, r=RUN),
         )
         make_identity(nc, identity[:])
-        gn_turned = psum.tile([P, P], F32, name="gn_turned", tag="b3")
+        gn_turned = psum.tile([P, P], F32, name="gn_turned", tag="upper%d" % LAST)
         nc.tensor.transpose(gn_turned[:], gn_rows[:], identity[:])
         gain = keep.tile([P, PACK], F32, name="gain")
         nc.scalar.activation(gain[:], gn_turned[:, 0:PACK], COPY, scale=CONST)
 
-        def coded_product(name, d_list, x_list, base):
-            d_picked_bytes = shared.tile([P, H], U8, name=name + "_d_bytes", offset=base + 4 * H - H // 2)
-            x_picked_bytes = keep.tile([P, S], U8, name=name + "_x_bytes", tag=name + "_x_bytes")
-            staged = keep.tile([P, H + S], U8, name=name + "_staged", tag=name + "_staged")
+        def coded_product(name, d_list, x_list, words_at, bytes_at, bank_tags):
+            pieces = len(bank_tags)
+            width = S // pieces
+
+            d_picked_bytes = shared.tile([P, H], U8, name=name + "_d_bytes", offset=bytes_at)
+            x_picked_bytes = keep.tile([P, S], U8, name=name + "_x_bytes")
+            staged = keep.tile([P, H + S], U8, name=name + "_staged")
             planes = keep.tile([P, H + S], U8, name=name + "_planes", align_bytes=64)
             nc.gpsimd.memset(planes[:].bitcast(I32), 0)
             nc.vector.tensor_copy(x_picked_bytes[:], x_bytes[:].indirect(x_list[:]))
             nc.vector.tensor_copy(d_picked_bytes[:], d_bytes[:].indirect(d_list[:]))
             nc.vector.tensor_copy(staged[:, H : H + S].bitcast(I32), x_picked_bytes[:].bitcast(I32))
             nc.vector.tensor_copy(
-                staged[:, 0:H].bitcast(I32).rearrange("p (t g r) -> p t g r", t=PACK, r=RUN // 4),
-                d_picked_bytes[:].bitcast(I32).rearrange("p (g t r) -> p t g r", t=PACK, r=RUN // 4),
+                staged[:, 0:H].bitcast(I32).rearrange("p (t g r) -> p t g r", t=PACK, r=RUN // PACK),
+                d_picked_bytes[:].bitcast(I32).rearrange("p (g t r) -> p t g r", t=PACK, r=RUN // PACK),
             )
-            for q in range(0, P, 32):
-                nc.sync.dma_start(planes[q : q + 4, :].bitcast(I32), staged[q : q + 32 : RUN, :].bitcast(I32))
-            d_picked = shared.tile([P, H], U32, name=name + "_d_words", offset=base)
-            d_dealt = keep.tile([P, H], U32, name=name + "_d_dealt", tag=name + "_d_dealt", align_bytes=64)
-            x_picked = shared.tile([P, S], U32, name=name + "_x_words", offset=base + 4 * H, align_bytes=64)
+            for q in range(0, P, QUADRANT):
+                nc.sync.dma_start(
+                    planes[q : q + QUADRANT // RUN, :].bitcast(I32), staged[q : q + QUADRANT : RUN, :].bitcast(I32)
+                )
+
+            d_picked = shared.tile([P, H], U32, name=name + "_d_words", offset=words_at)
+            d_dealt = keep.tile([P, H], U32, name=name + "_d_dealt", align_bytes=64)
+            x_picked = shared.tile([P, S], U32, name=name + "_x_words", offset=words_at + WORDS, align_bytes=64)
             nc.vector.tensor_copy(d_picked[:], d_table[:].indirect(d_list[:]))
-            nc.vector.tensor_copy(x_picked[:], x_table[:].indirect(x_list[:]))
+            for piece in range(pieces):
+                entries = x_list[:, piece * width // LIST_ROWS : (piece + 1) * width // LIST_ROWS]
+                nc.vector.tensor_copy(x_picked[:, piece * width : (piece + 1) * width], x_table[:].indirect(entries))
             nc.vector.tensor_copy(
                 d_dealt[:].rearrange("p (t g r) -> p t g r", t=PACK, r=RUN),
                 d_picked[:].rearrange("p (g t r) -> p t g r", t=PACK, r=RUN),
             )
-            banks = []
-            for t in range(PACK):
-                bank = psum.tile([P, S], F32, name=name + str(t), tag=name + str(t))
-                cols = slice(t * P, (t + 1) * P)
-                nc.tensor.matmul_mx(
-                    out=bank[:],
-                    lhsT=d_dealt[:, cols].bitcast(FP8X4),
-                    lhsT_scale=planes[:, cols],
-                    rhs=x_picked[:].bitcast(FP8X4),
-                    rhs_scale=planes[:, H : H + S],
-                    start=True,
-                    stop=True,
-                )
-                banks.append(bank)
+
+            banks = {}
+            for piece in range(pieces):
+                for t in range(PACK):
+                    bank = psum.tile([P, width], F32, name="%s%d%d" % (name, piece, t), tag=bank_tags[piece] + str(t))
+                    d_cols = slice(t * P, (t + 1) * P)
+                    nc.tensor.matmul_mx(
+                        out=bank[:],
+                        lhsT=d_dealt[:, d_cols].bitcast(FP8X4),
+                        lhsT_scale=planes[:, d_cols],
+                        rhs=x_picked[:, piece * width : (piece + 1) * width].bitcast(FP8X4),
+                        rhs_scale=planes[:, H + piece * width : H + (piece + 1) * width],
+                        start=True,
+                        stop=True,
+                    )
+                    banks[piece, t] = bank
             return banks
 
-        a_banks = coded_product("a", k1_l, offs_l, 0)
-        w_raw = keep.tile([P, PACK, N], F32, name="w_raw", tag="a_staged")
+        a_banks = coded_product("a", k1_list, offs_list, A_WORDS_AT, A_BYTES_AT, ("lower", "upper"))
+
+        w_raw = shared.tile([P, PACK, N], F32, name="w_raw", offset=A_BYTES_AT)
         w_rows = w1.rearrange("(g t r) n -> t g r n", t=PACK, r=RUN)
         for t in range(PACK):
             nc.sync.dma_start(w_raw[:, t, :], w_rows[t])
-        b_banks = coded_product("b", k2_l, two_l, 4 * (H + S))
+
+        b_banks = coded_product("b", k2_list, two_list, B_WORDS_AT, B_BYTES_AT, ("upper",))
 
         def half_cols(half):
             return slice(half * HALF, (half + 1) * HALF)
 
-        def looked_up(window, lists, half):
-            return window[:].indirect(lists[:, half * LIST_HALF : (half + 1) * LIST_HALF])
+        def looked_up(window, places, half):
+            return window[:].indirect(places[:, half * HALF // LIST_ROWS : (half + 1) * HALF // LIST_ROWS])
 
         a_rows = [keep.tile([P, S], F32, name="a_rows%d" % t) for t in range(PACK)]
         b_rows = [keep.tile([P, S], F32, name="b_rows%d" % t) for t in range(PACK)]
         h_rows = [keep.tile([P, S], F32, name="h_rows%d" % t) for t in range(PACK)]
-        for t in range(PACK):
-            nc.scalar.activation(a_rows[t][:], a_banks[t][:], COPY, scale=gain[:, t : t + 1])
+        for half in range(2):
+            for t in range(PACK):
+                nc.scalar.activation(a_rows[t][:, half_cols(half)], a_banks[half, t][:], COPY, scale=gain[:, t : t + 1])
 
-        def fetch(engine, name, rows, lists, half, t):
+        def fetch(engine, name, rows, places, half, t):
             far = keep.tile([P, HALF], F32, name="%s_far%d%d" % (name, half, t))
             if engine is nc.scalar:
-                nc.scalar.activation(far[:], looked_up(rows[t], lists, half), COPY)
+                nc.scalar.activation(far[:], looked_up(rows[t], places, half), COPY)
             else:
-                nc.vector.tensor_copy(far[:], looked_up(rows[t], lists, half))
+                nc.vector.tensor_copy(far[:], looked_up(rows[t], places, half))
             return far
 
         plus = [keep.tile([P, PACK, HALF], F32, name="plus%d" % half) for half in range(2)]
         minus = [keep.tile([P, PACK, HALF], F32, name="minus%d" % half) for half in range(2)]
         h_banks = {}
 
-        def make_minus(half, t, a_far):
-            nc.vector.tensor_tensor(minus[half][:, t, :], b_banks[t][:, half_cols(half)], a_far[:], MULT)
+        def make_minus(half, t, a_looked_up):
+            nc.vector.tensor_tensor(minus[half][:, t, :], b_banks[0, t][:, half_cols(half)], a_looked_up[:], MULT)
 
         def make_plus(half, t):
-            b_far = fetch(nc.scalar, "b", b_rows, n2_l, half, t)
+            b_far = fetch(nc.scalar, "b", b_rows, n2_list, half, t)
             nc.vector.tensor_tensor(plus[half][:, t, :], b_far[:], a_rows[t][:, half_cols(half)], MULT)
 
-        def dense_layer(half):
+        def dense_layer(half, bank_tag):
             z_grouped = keep.tile([P, HALF, PACK], BF16, name="z_grouped%d" % half, align_bytes=64)
             nc.vector.tensor_tensor(
-                z_grouped[:].rearrange("p (c i) t -> p c t i", i=4),
-                plus[half][:].rearrange("p t (c i) -> p c t i", i=4),
-                minus[half][:].rearrange("p t (c i) -> p c t i", i=4),
+                z_grouped[:].rearrange("p (c i) t -> p c t i", i=LINE),
+                plus[half][:].rearrange("p t (c i) -> p c t i", i=LINE),
+                minus[half][:].rearrange("p t (c i) -> p c t i", i=LINE),
                 SUB,
             )
             z_codes = keep.tile([P, HALF], U32, name="z_codes%d" % half, align_bytes=64)
@@ -163,7 +191,7 @@ def tile_picked_twpqcrossbdif_none_p_kernel(tc, x_words, x_scales, d_words, d_sc
                 out=z_codes[:].bitcast(FP8X4), scales=z_scales[:], in_=z_grouped[:].rearrange("p c t -> p (c t)")
             )
             for t in range(PACK):
-                bank = psum.tile([P, HALF], F32, name="h%d%d" % (half, t), tag="ab"[half] + str(t))
+                bank = psum.tile([P, HALF], F32, name="h%d%d" % (half, t), tag=bank_tag + str(t))
                 w_cols = slice(t * P, (t + 1) * P)
                 nc.tensor.matmul_mx(
                     out=bank[:],
@@ -176,51 +204,56 @@ def tile_picked_twpqcrossbdif_none_p_kernel(tc, x_words, x_scales, d_words, d_sc
                 )
                 h_banks[half, t] = bank
 
-        last = PACK - 1
+        a_far = {(0, t): fetch(nc.scalar, "a", a_rows, n1_list, 0, t) for t in range(PACK)}
+        for t in range(EARLY):
+            a_far[1, t] = fetch(nc.scalar, "a", a_rows, n1_list, 1, t)
 
-        def make_plus_fused(half, t):
-            nc.vector.tensor_tensor(plus[half][:, t, :], looked_up(b_rows[t], n2_l, half), a_rows[t][:, half_cols(half)], MULT)
-
-        a_far = {(0, t): fetch(nc.scalar, "a", a_rows, n1_l, 0, t) for t in range(PACK)}
-        a_far[1, 0] = fetch(nc.scalar, "a", a_rows, n1_l, 1, 0)
-        w_grouped = shared.tile([P, PACK, P, PACK], BF16, name="w_grouped", offset=4 * H, align_bytes=64)
+        w_grouped = shared.tile([P, PACK, P, PACK], BF16, name="w_grouped", offset=W_GROUPED_AT, align_bytes=64)
         for t in range(PACK):
             nc.vector.tensor_copy(
-                w_grouped[:, t].rearrange("p (g s i) j -> p g s j i", s=2, i=4),
-                w_raw[:].rearrange("p j (g t s i) -> p t g s j i", t=PACK, s=2, i=4)[:, t],
+                w_grouped[:, t].rearrange("p (g s i) j -> p g s j i", s=RUN // LINE, i=LINE),
+                w_raw[:].rearrange("p j (g t s i) -> p t g s j i", t=PACK, s=RUN // LINE, i=LINE)[:, t],
             )
         w_codes = keep.tile([P, N], U32, name="w_codes", align_bytes=64)
         w_scales = keep.tile([P, N], U8, name="w_scales", align_bytes=64)
-
         nc.vector.quantize_mx(
             out=w_codes[:].bitcast(FP8X4), scales=w_scales[:], in_=w_grouped[:].rearrange("p t m j -> p (t m j)")
         )
+
         for t in range(PACK):
-            nc.scalar.copy(b_rows[t][:], b_banks[t][:])
+            nc.scalar.copy(b_rows[t][:], b_banks[0, t][:])
             make_minus(0, t, a_far[0, t])
-            if t < last:
-                make_plus(0, t)
-        make_minus(1, 0, a_far[1, 0])
-        make_plus_fused(0, last)
-        dense_layer(0)
-        for t in range(1, PACK):
-            make_minus(1, t, fetch(nc.scalar, "a", a_rows, n1_l, 1, t))
-        make_plus_fused(1, last)
-        for t in range(last):
+            make_plus(0, t)
+        for t in range(EARLY):
+            make_minus(1, t, a_far[1, t])
+        dense_layer(0, "lower")
+
+        for t in range(EARLY, PACK):
+            make_minus(1, t, fetch(nc.scalar, "a", a_rows, n1_list, 1, t))
+        nc.vector.tensor_tensor(
+            plus[1][:, LAST, :], looked_up(b_rows[LAST], n2_list, 1), a_rows[LAST][:, half_cols(1)], MULT
+        )
+        for t in range(LAST):
             make_plus(1, t)
         for t in range(PACK):
             nc.scalar.copy(h_rows[t][:, half_cols(0)], h_banks[0, t][:])
-        dense_layer(1)
+        dense_layer(1, "upper")
+
         for t in range(PACK):
             if t % 2 == 1:
                 nc.vector.tensor_copy(h_rows[t][:, half_cols(1)], h_banks[1, t][:])
             else:
                 nc.scalar.copy(h_rows[t][:, half_cols(1)], h_banks[1, t][:])
-
         out_rows = out.rearrange("(g t r) n -> t g r n", t=PACK, r=RUN)
-        for t in range(PACK):
+        for pair in range(0, PACK, 2):
             for half in range(2):
-                h_far = fetch(nc.vector if t == 1 else nc.scalar, "h", h_rows, n3_l, half, t)
-                result = keep.tile([P, HALF], F32, name="result%d%d" % (half, t))
-                nc.vector.tensor_tensor(result[:], h_banks[half, t][:], h_far[:], SUB)
-                nc.sync.dma_start(out_rows[t][:, :, half_cols(half)], result[:])
+                for t in (pair, pair + 1):
+                    closing = pair + 1 == LAST and half == 1
+                    on_vector = t % 2 == 1 and not closing
+                    h_far = fetch(nc.vector if on_vector else nc.scalar, "h", h_rows, n3_list, half, t)
+                    result = keep.tile([P, HALF], F32, name="result%d%d" % (half, t))
+                    if t % 2 == 0 and not closing:
+                        nc.gpsimd.tensor_tensor(result[:], h_rows[t][:, half_cols(half)], h_far[:], SUB)
+                    else:
+                        nc.vector.tensor_tensor(result[:], h_banks[half, t][:], h_far[:], SUB)
+                    nc.sync.dma_start(out_rows[t][:, :, half_cols(half)], result[:])

from contextlib import ExitStack

import concourse.mybir as mybir
from concourse.masks import make_identity

K, T, S, N, G, H = 512, 1024, 512, 512, 2048, 512
FLOPS = 2 * K * H * S * 2 + 2 * H * N * S

F32 = mybir.dt.float32
BF16 = mybir.dt.bfloat16
I32 = mybir.dt.int32
U32 = mybir.dt.uint32
U16 = mybir.dt.uint16
U8 = mybir.dt.uint8
FP8X4 = mybir.dt.float8_e4m3fn_x4
COPY = mybir.ActivationFunctionType.Copy
MULT = mybir.AluOpType.mult
SUB = mybir.AluOpType.subtract

P = 128
QUADRANT = 32
PACK = 4
RUN = 8
LIST_ROWS = 16
SCALE_ROWS = K // 32
LINE = 4
HALF = S // 2
LAST = PACK - 1
CONST = 0.75 * 0.0625 * 0.0625
EARLY = 2

WORDS = PACK * H
A_WORDS_AT = 0
B_WORDS_AT = 2 * WORDS
A_BYTES_AT = 4 * WORDS
B_BYTES_AT = B_WORDS_AT + WORDS - H // 2
W_GROUPED_AT = A_WORDS_AT + WORDS


def tile_picked_twpqcrossbdif_none_p_kernel(tc, x_words, x_scales, d_words, d_scales, gn, w1, offs, k1, two, k2, n1, n2, n3, out):
    nc = tc.nc
    with ExitStack() as ctx:
        keep = ctx.enter_context(tc.tile_pool(name="keep", bufs=1))
        shared = ctx.enter_context(tc.tile_pool(name="shared", bufs=1))
        psum = ctx.enter_context(tc.psum_pool(name="psum", bufs=1))

        def load_list(src, name):
            tile = keep.tile([P, S // LIST_ROWS], U16, name=name)
            nc.sync.dma_start(tile[:], src)
            return tile

        def scale_rows(scales):
            rows = scales[0].bitcast(I32)
            return rows.unsqueeze(1).to_broadcast([SCALE_ROWS, RUN, rows.shape[1]])

        def packed_words(words):
            return words[0].rearrange("p n t -> p (n t)").bitcast(I32)

        d_bytes = keep.tile([P, G], U8, name="d_bytes")
        x_bytes = keep.tile([P, T], U8, name="x_bytes")
        d_table = keep.tile([P, G], U32, name="d_table")
        x_table = keep.tile([P, T], U32, name="x_table")

        nc.sync.dma_start(x_bytes[:].bitcast(I32), scale_rows(x_scales))
        offs_list = load_list(offs, "offs_list")
        nc.sync.dma_start(d_bytes[:].bitcast(I32), scale_rows(d_scales))
        k1_list = load_list(k1, "k1_list")
        nc.sync.dma_start(d_table[:].bitcast(I32), packed_words(d_words))
        n1_list = load_list(n1, "n1_list")
        n2_list = load_list(n2, "n2_list")
        nc.sync.dma_start(x_table[:].bitcast(I32), packed_words(x_words))
        two_list = load_list(two, "two_list")
        k2_list = load_list(k2, "k2_list")
        n3_list = load_list(n3, "n3_list")

        gn_rows = keep.tile([P, P], F32, name="gn_rows")
        identity = keep.tile([P, P], F32, name="identity")
        nc.gpsimd.memset(gn_rows[:], 0.0)
        nc.scalar.dma_start(
            gn_rows[0:PACK, :].rearrange("t (g r) -> t g r", r=RUN),
            gn.rearrange("(g t r) o -> t g (r o)", t=PACK, r=RUN),
        )
        make_identity(nc, identity[:])
        gn_turned = psum.tile([P, P], F32, name="gn_turned", tag="upper%d" % LAST)
        nc.tensor.transpose(gn_turned[:], gn_rows[:], identity[:])
        gain = keep.tile([P, PACK], F32, name="gain")
        nc.scalar.activation(gain[:], gn_turned[:, 0:PACK], COPY, scale=CONST)

        def coded_product(name, d_list, x_list, words_at, bytes_at, bank_tags):
            pieces = len(bank_tags)
            width = S // pieces

            d_picked_bytes = shared.tile([P, H], U8, name=name + "_d_bytes", offset=bytes_at)
            x_picked_bytes = keep.tile([P, S], U8, name=name + "_x_bytes")
            staged = keep.tile([P, H + S], U8, name=name + "_staged")
            planes = keep.tile([P, H + S], U8, name=name + "_planes", align_bytes=64)
            nc.gpsimd.memset(planes[:].bitcast(I32), 0)
            nc.vector.tensor_copy(x_picked_bytes[:], x_bytes[:].indirect(x_list[:]))
            nc.vector.tensor_copy(d_picked_bytes[:], d_bytes[:].indirect(d_list[:]))
            nc.vector.tensor_copy(staged[:, H : H + S].bitcast(I32), x_picked_bytes[:].bitcast(I32))
            nc.vector.tensor_copy(
                staged[:, 0:H].bitcast(I32).rearrange("p (t g r) -> p t g r", t=PACK, r=RUN // PACK),
                d_picked_bytes[:].bitcast(I32).rearrange("p (g t r) -> p t g r", t=PACK, r=RUN // PACK),
            )
            for q in range(0, P, QUADRANT):
                nc.sync.dma_start(
                    planes[q : q + QUADRANT // RUN, :].bitcast(I32), staged[q : q + QUADRANT : RUN, :].bitcast(I32)
                )

            d_picked = shared.tile([P, H], U32, name=name + "_d_words", offset=words_at)
            d_dealt = keep.tile([P, H], U32, name=name + "_d_dealt", align_bytes=64)
            x_picked = shared.tile([P, S], U32, name=name + "_x_words", offset=words_at + WORDS, align_bytes=64)
            nc.vector.tensor_copy(d_picked[:], d_table[:].indirect(d_list[:]))
            for piece in range(pieces):
                entries = x_list[:, piece * width // LIST_ROWS : (piece + 1) * width // LIST_ROWS]
                nc.vector.tensor_copy(x_picked[:, piece * width : (piece + 1) * width], x_table[:].indirect(entries))
            nc.vector.tensor_copy(
                d_dealt[:].rearrange("p (t g r) -> p t g r", t=PACK, r=RUN),
                d_picked[:].rearrange("p (g t r) -> p t g r", t=PACK, r=RUN),
            )

            banks = {}
            for piece in range(pieces):
                for t in range(PACK):
                    bank = psum.tile([P, width], F32, name="%s%d%d" % (name, piece, t), tag=bank_tags[piece] + str(t))
                    d_cols = slice(t * P, (t + 1) * P)
                    nc.tensor.matmul_mx(
                        out=bank[:],
                        lhsT=d_dealt[:, d_cols].bitcast(FP8X4),
                        lhsT_scale=planes[:, d_cols],
                        rhs=x_picked[:, piece * width : (piece + 1) * width].bitcast(FP8X4),
                        rhs_scale=planes[:, H + piece * width : H + (piece + 1) * width],
                        start=True,
                        stop=True,
                    )
                    banks[piece, t] = bank
            return banks

        a_banks = coded_product("a", k1_list, offs_list, A_WORDS_AT, A_BYTES_AT, ("lower", "upper"))

        w_raw = shared.tile([P, PACK, N], F32, name="w_raw", offset=A_BYTES_AT)
        w_rows = w1.rearrange("(g t r) n -> t g r n", t=PACK, r=RUN)
        for t in range(PACK):
            nc.sync.dma_start(w_raw[:, t, :], w_rows[t])

        b_banks = coded_product("b", k2_list, two_list, B_WORDS_AT, B_BYTES_AT, ("upper",))

        def half_cols(half):
            return slice(half * HALF, (half + 1) * HALF)

        def looked_up(window, places, half):
            return window[:].indirect(places[:, half * HALF // LIST_ROWS : (half + 1) * HALF // LIST_ROWS])

        a_rows = [keep.tile([P, S], F32, name="a_rows%d" % t) for t in range(PACK)]
        b_rows = [keep.tile([P, S], F32, name="b_rows%d" % t) for t in range(PACK)]
        h_rows = [keep.tile([P, S], F32, name="h_rows%d" % t) for t in range(PACK)]
        for half in range(2):
            for t in range(PACK):
                nc.scalar.activation(a_rows[t][:, half_cols(half)], a_banks[half, t][:], COPY, scale=gain[:, t : t + 1])

        def fetch(engine, name, rows, places, half, t):
            far = keep.tile([P, HALF], F32, name="%s_far%d%d" % (name, half, t))
            if engine is nc.scalar:
                nc.scalar.activation(far[:], looked_up(rows[t], places, half), COPY)
            else:
                nc.vector.tensor_copy(far[:], looked_up(rows[t], places, half))
            return far

        plus = [keep.tile([P, PACK, HALF], F32, name="plus%d" % half) for half in range(2)]
        minus = [keep.tile([P, PACK, HALF], F32, name="minus%d" % half) for half in range(2)]
        h_banks = {}

        def make_minus(half, t, a_looked_up):
            nc.vector.tensor_tensor(minus[half][:, t, :], b_banks[0, t][:, half_cols(half)], a_looked_up[:], MULT)

        def make_plus(half, t):
            b_far = fetch(nc.scalar, "b", b_rows, n2_list, half, t)
            nc.vector.tensor_tensor(plus[half][:, t, :], b_far[:], a_rows[t][:, half_cols(half)], MULT)

        def dense_layer(half, bank_tag):
            z_grouped = keep.tile([P, HALF, PACK], BF16, name="z_grouped%d" % half, align_bytes=64)
            nc.vector.tensor_tensor(
                z_grouped[:].rearrange("p (c i) t -> p c t i", i=LINE),
                plus[half][:].rearrange("p t (c i) -> p c t i", i=LINE),
                minus[half][:].rearrange("p t (c i) -> p c t i", i=LINE),
                SUB,
            )
            z_codes = keep.tile([P, HALF], U32, name="z_codes%d" % half, align_bytes=64)
            z_scales = keep.tile([P, HALF], U8, name="z_scales%d" % half, align_bytes=64)
            nc.vector.quantize_mx(
                out=z_codes[:].bitcast(FP8X4), scales=z_scales[:], in_=z_grouped[:].rearrange("p c t -> p (c t)")
            )
            for t in range(PACK):
                bank = psum.tile([P, HALF], F32, name="h%d%d" % (half, t), tag=bank_tag + str(t))
                w_cols = slice(t * P, (t + 1) * P)
                nc.tensor.matmul_mx(
                    out=bank[:],
                    lhsT=w_codes[:, w_cols].bitcast(FP8X4),
                    lhsT_scale=w_scales[:, w_cols],
                    rhs=z_codes[:].bitcast(FP8X4),
                    rhs_scale=z_scales[:],
                    start=True,
                    stop=True,
                )
                h_banks[half, t] = bank

        a_far = {(0, t): fetch(nc.scalar, "a", a_rows, n1_list, 0, t) for t in range(PACK)}
        for t in range(EARLY):
            a_far[1, t] = fetch(nc.scalar, "a", a_rows, n1_list, 1, t)

        w_grouped = shared.tile([P, PACK, P, PACK], BF16, name="w_grouped", offset=W_GROUPED_AT, align_bytes=64)
        for t in range(PACK):
            nc.vector.tensor_copy(
                w_grouped[:, t].rearrange("p (g s i) j -> p g s j i", s=RUN // LINE, i=LINE),
                w_raw[:].rearrange("p j (g t s i) -> p t g s j i", t=PACK, s=RUN // LINE, i=LINE)[:, t],
            )
        w_codes = keep.tile([P, N], U32, name="w_codes", align_bytes=64)
        w_scales = keep.tile([P, N], U8, name="w_scales", align_bytes=64)
        nc.vector.quantize_mx(
            out=w_codes[:].bitcast(FP8X4), scales=w_scales[:], in_=w_grouped[:].rearrange("p t m j -> p (t m j)")
        )

        for t in range(PACK):
            nc.scalar.copy(b_rows[t][:], b_banks[0, t][:])
            make_minus(0, t, a_far[0, t])
            make_plus(0, t)
        for t in range(EARLY):
            make_minus(1, t, a_far[1, t])
        dense_layer(0, "lower")

        for t in range(EARLY, PACK):
            make_minus(1, t, fetch(nc.scalar, "a", a_rows, n1_list, 1, t))
        nc.vector.tensor_tensor(
            plus[1][:, LAST, :], looked_up(b_rows[LAST], n2_list, 1), a_rows[LAST][:, half_cols(1)], MULT
        )
        for t in range(LAST):
            make_plus(1, t)
        for t in range(PACK):
            nc.scalar.copy(h_rows[t][:, half_cols(0)], h_banks[0, t][:])
        dense_layer(1, "upper")

        for t in range(PACK):
            if t % 2 == 1:
                nc.vector.tensor_copy(h_rows[t][:, half_cols(1)], h_banks[1, t][:])
            else:
                nc.scalar.copy(h_rows[t][:, half_cols(1)], h_banks[1, t][:])
        out_rows = out.rearrange("(g t r) n -> t g r n", t=PACK, r=RUN)
        for pair in range(0, PACK, 2):
            for half in range(2):
                for t in (pair, pair + 1):
                    closing = pair + 1 == LAST and half == 1
                    on_vector = t % 2 == 1 and not closing
                    h_far = fetch(nc.vector if on_vector else nc.scalar, "h", h_rows, n3_list, half, t)
                    result = keep.tile([P, HALF], F32, name="result%d%d" % (half, t))
                    if t % 2 == 0 and not closing:
                        nc.gpsimd.tensor_tensor(result[:], h_rows[t][:, half_cols(half)], h_far[:], SUB)
                    else:
                        nc.vector.tensor_tensor(result[:], h_banks[half, t][:], h_far[:], SUB)
                    nc.sync.dma_start(out_rows[t][:, :, half_cols(half)], result[:])
